import numpy as np
import ml_dtypes


def mxq(x, axis, fmt="e4m3"):
    dtype, down = {"e4m3": (ml_dtypes.float8_e4m3fn, 7), "e5m2": (ml_dtypes.float8_e5m2, 14)}[fmt]
    v = np.moveaxis(np.asarray(x, np.float32).astype(ml_dtypes.bfloat16).astype(np.float64), axis, -1)
    blocks = v.reshape(v.shape[:-1] + (-1, 32))
    amax = np.abs(blocks).max(-1, keepdims=True)
    byte = np.maximum(np.where(amax > 0, np.frexp(amax)[1] - 1 + 127, 0) - down, 1)
    scale = np.exp2(byte - 127.0)
    codes = (blocks / scale).astype(np.float32).astype(dtype).astype(np.float64)
    return np.moveaxis((codes * scale).reshape(v.shape), -1, axis)


WIDE = False


def mx_kscale(k):
    if not WIDE:
        return np.ones(k)
    levels = np.array([10, -10, 5, -5, 0])
    if k % 512:
        return np.exp2(np.random.permutation(np.resize(levels, k // 32))).repeat(32)
    a = np.empty((k // 512, 16))
    for p in range(k // 512):
        a[p, :8] = np.random.permutation(np.resize(levels, 8))
        for g in range(8):
            far = levels[np.abs(levels - a[p, g]) >= 10]
            a[p, g + 8] = far[np.random.randint(len(far))]
    return np.exp2(a.ravel()).repeat(32)


def f64(x):
    return np.asarray(x).astype(np.float64)


def striped(idx):
    return np.tile(idx.reshape(-1, 16).T, (8, 1)).astype(np.uint16)


def unstriped(offs):
    return offs[:16].T.reshape(-1).astype(np.int64)


E2M1 = np.array([0.0, 0.5, 1.0, 1.5, 2.0, 3.0, 4.0, 6.0, -0.0, -0.5, -1.0, -1.5, -2.0, -3.0, -4.0, -6.0])


def pack_weight(w, fmt):
    k, n = w.shape
    w = f64(np.asarray(w, np.float32).astype(ml_dtypes.bfloat16)).reshape(k // 32, 32, n)
    amax = np.abs(w).max(1)
    if fmt == "e4m3":
        byte = np.frexp(amax)[1] - 1 + 127 - 7
    else:
        mant, ex = np.frexp(amax / 6.0)
        byte = np.where(mant > 0.5, ex, ex - 1) + 127
    byte = np.clip(np.where(amax > 0, byte, 1), 1, 254)
    scaled = (w * np.exp2(127.0 - byte)[:, None, :]).reshape(k, n).astype(np.float32)
    by_word = np.ascontiguousarray(scaled.reshape(k // 512, 128, 4, n).transpose(0, 1, 3, 2))
    if fmt == "e4m3":
        words = by_word.astype(ml_dtypes.float8_e4m3fn).view(np.uint8)
    else:
        c = by_word.astype(ml_dtypes.float4_e2m1fn).view(np.uint8) & 0xF
        words = (c[..., 0::2] | (c[..., 1::2] << 4)).reshape(k // 512, 128, 2 * n)
    return np.ascontiguousarray(words), np.ascontiguousarray(byte.astype(np.uint8).reshape(k // 512, 16, n))


def unpack_weight(words, scales, fmt):
    g, _, n = scales.shape
    words = np.ascontiguousarray(words).reshape(g, 128, n, -1)
    if fmt == "e4m3":
        vals = words.view(ml_dtypes.float8_e4m3fn).astype(np.float64)
    else:
        nib = np.empty((g, 128, n, 4), np.uint8)
        nib[..., 0::2] = words & 0xF
        nib[..., 1::2] = words >> 4
        vals = E2M1[nib]
    vals = vals * np.repeat(np.exp2(scales.astype(np.float64) - 127.0), 8, axis=1)[..., None]
    return vals.transpose(0, 1, 3, 2).reshape(g * 512, n)


def gelu(v):
    return 0.5 * v * (1.0 + np.tanh(np.sqrt(2.0 / np.pi) * (v + 0.044715 * v**3)))


K, T, S, K2, H, N = 1024, 4096, 1024, 512, 1024, 512

def setup_inputs():
    n = np.random.standard_normal
    s = mx_kscale(K)[:, None]
    s2 = mx_kscale(K2)[:, None]
    u = mx_kscale(H)[:, None]
    d = {}
    d["tab_words"], d["tab_scales"] = pack_weight(n((K, T)) * s, "e4m3")
    d["offs"] = striped(np.random.permutation(T)[:S])
    d["xs_words"], d["xs_scales"] = pack_weight(n((K2, S)) * s2, "e4m3")
    d["w1"] = (n((K, H)) / s * u.T / K ** 0.5).astype(np.float32)
    d["w2_words"], d["w2_scales"] = pack_weight(n((K2, H)) / s2 * u.T / K2 ** 0.5, "e2m1")
    d["reserve"] = (0.7 * n(H) * u[:, 0]).astype(np.float32)
    d["w3"] = (n((H, N)) / u / H ** 0.5).astype(np.float32)
    d["w4_words"], d["w4_scales"] = pack_weight(n((H, N)) / u / H ** 0.5, "e4m3")
    d["base"] = (0.5 * n(N)).astype(np.float32)
    return d

def reference(tab_words, tab_scales, offs, xs_words, xs_scales, w1, w2_words, w2_scales,
              reserve, w3, w4_words, w4_scales, base):
    v = unpack_weight(tab_words, tab_scales, "e4m3")[:, unstriped(offs)]
    xs = unpack_weight(xs_words, xs_scales, "e4m3")
    w2 = unpack_weight(w2_words, w2_scales, "e2m1")
    w4 = unpack_weight(w4_words, w4_scales, "e4m3")
    demand = mxq(f64(w1), 0, "e4m3").T @ v
    supply = w2.T @ xs
    gap = demand - supply + f64(reserve)[:, None]
    short = np.maximum(gap, 0.0)
    over = np.maximum(-gap, 0.0)
    ys = mxq(f64(w3), 0, "e4m3").T @ mxq(short, 0, "e4m3")
    yo = w4.T @ mxq(over, 0, "e4m3")
    return ys - yo + f64(base)[:, None]

@@ -1,0 +1,269 @@
+from contextlib import ExitStack
+
+import concourse.mybir as mybir
+
+K, T, S, K2, H, N = 1024, 4096, 1024, 512, 1024, 512
+FLOPS = 2 * S * (K * H + K2 * H + 2 * H * N)
+
+F32 = mybir.dt.float32
+BF16 = mybir.dt.bfloat16
+I32 = mybir.dt.int32
+U32 = mybir.dt.uint32
+U16 = mybir.dt.uint16
+U8 = mybir.dt.uint8
+FP8X4 = mybir.dt.float8_e4m3fn_x4
+FP4X4 = mybir.dt.float4_e2m1fn_x4
+ALU = mybir.AluOpType
+ACT = mybir.ActivationFunctionType
+
+P = 128
+PACK = 4
+PASS = P * PACK
+HALF = 512
+
+
+def tile_list_fleet_shortage_surplus_kernel(
+    tc, tab_words, tab_scales, offs, xs_words, xs_scales, w1, w2_words, w2_scales,
+    reserve, w3, w4_words, w4_scales, base, out,
+):
+    nc = tc.nc
+    with ExitStack() as ctx:
+        keep = ctx.enter_context(tc.tile_pool(name="keep", bufs=1))
+        ring = ctx.enter_context(tc.tile_pool(name="ring", bufs=2))
+        psum = ctx.enter_context(tc.psum_pool(name="psum", bufs=1))
+
+        def tile(name, shape, dtype):
+            return keep.tile(shape, dtype, name=name, align_bytes=64)
+
+        def bank(i):
+            return psum.tile([P, HALF], F32, name="bank%d" % i)
+
+        def words(ap):
+            return ap.rearrange("p c i -> p (c i)").bitcast(I32)
+
+        def zeroed_plane(name, width):
+            plane = tile(name, [P, width], U8)
+            nc.vector.memset(plane[:].bitcast(I32), 0)
+            return plane
+
+        def load_plane(queue, plane, scales):
+            passes = scales.shape[0]
+            for q in range(4):
+                src = scales[:, 4 * q : 4 * q + 4, :] if passes > 1 else scales[0, 4 * q : 4 * q + 4, :]
+                queue.dma_start(out=plane[32 * q : 32 * q + 4 * passes, :].bitcast(I32), in_=src.bitcast(I32))
+
+        def move_rows(plane, rows, passes=1):
+            for q in range(4):
+                live = slice(32 * q, 32 * q + 4 * passes)
+                nc.vector.tensor_copy(out=plane[live, :].bitcast(I32), in_=rows[live, :].bitcast(I32))
+
+        def load_rows(name, w, a, c0, c1):
+            raw = tile(name, [P, PACK, c1 - c0], F32)
+            nc.sync.dma_start(out=raw[:], in_=w[a * PASS : (a + 1) * PASS, c0:c1].rearrange("(p j) c -> p j c", j=PACK))
+            return raw
+
+        def quantise(name, grouped, pieces=1):
+            width = grouped.shape[1] // PACK
+            codes = tile(name + "_codes", [P, width], U32)
+            plane = tile(name + "_plane", [P, width], U8)
+            step = width // pieces
+            for c in range(0, width, step):
+                nc.vector.quantize_mx(
+                    out=codes[:, c : c + step].bitcast(FP8X4),
+                    scales=plane[:, c : c + step],
+                    in_=grouped[:, PACK * c : PACK * (c + step)],
+                )
+            return codes, plane
+
+        xs_plane = zeroed_plane("xs_plane", S)
+        tab_plane = zeroed_plane("tab_plane", T)
+        w2_plane_raw = zeroed_plane("w2_plane_raw", H)
+        w4_plane = zeroed_plane("w4_plane", N)
+        w2_rows = tile("w2_rows", [P, H], U8)
+        load_plane(nc.gpsimd, tab_plane, tab_scales)
+
+        w1_raw = {}
+        tab = [tile("tab%d" % a, [P, T], U32) for a in range(2)]
+        offsets = keep.tile([P, S // 16], U16, name="offsets")
+        w2_raw = tile("w2_raw", [P, 2 * H], U8)
+        xs = tile("xs", [P, S], U32)
+        res = tile("res", [P, 2, PACK], F32)
+        w4 = tile("w4", [P, 2, N], U32)
+        bias = tile("bias", [P, N // P], F32)
+
+        nc.sync.dma_start(out=w2_raw[:].bitcast(I32), in_=w2_words[0].bitcast(I32))
+        nc.sync.dma_start(offsets[:], offs)
+        load_plane(nc.sync, w2_rows, w2_scales)
+        for a in range(2):
+            nc.sync.dma_start(out=tab[a][:].bitcast(I32), in_=words(tab_words[a]))
+        load_plane(nc.sync, xs_plane, xs_scales)
+        nc.sync.dma_start(out=xs[:].bitcast(I32), in_=words(xs_words[0]))
+        w1_raw[0, 0] = [load_rows("w1_raw00", w1, 0, 0, PASS)]
+        w1_raw[1, 0] = [load_rows("w1_raw10_%d" % u, w1, 1, u * PASS // 2, (u + 1) * PASS // 2) for u in range(2)]
+        nc.sync.dma_start(out=res[:], in_=reserve.rearrange("(b p t) -> p b t", b=2, t=PACK))
+        w1_raw[0, 1] = [load_rows("w1_raw01", w1, 0, PASS, 2 * PASS)]
+        w1_raw[1, 1] = [load_rows("w1_raw11", w1, 1, PASS, 2 * PASS)]
+        w3_raw = [load_rows("w3_raw0", w3, 0, 0, N)]
+        load_plane(nc.sync, w4_plane, w4_scales)
+        nc.sync.dma_start(out=w4[:].bitcast(I32), in_=w4_words.rearrange("a p c i -> p a (c i)").bitcast(I32))
+        w3_raw.append(load_rows("w3_raw1", w3, 1, 0, N))
+        with nc.allow_non_contiguous_dma(reason="one value of base to a partition"):
+            nc.sync.dma_start(out=bias[:], in_=base.rearrange("(i p) -> p i", p=P))
+
+        def round_w1(a, b, engines):
+            grouped = tile("w1_grouped%d%d" % (a, b), [P, PASS * PACK], BF16)
+            share = P // len(engines)
+            for u, engine in enumerate(engines):
+                dst = grouped[:].rearrange("p (t m j) -> p m j t", t=PACK, j=PACK)[:, u * share : (u + 1) * share]
+                src = w1_raw[a, b][u][:].rearrange("p j (m t) -> p m j t", t=PACK)
+                if engine is nc.scalar:
+                    nc.scalar.activation(out=dst, in_=src, func=ACT.Copy, scale=-1.0)
+                else:
+                    nc.vector.tensor_scalar(out=dst, in0=src, scalar1=-1.0, scalar2=None, op0=ALU.mult)
+            return grouped
+
+        def round_w3(a, engine):
+            grouped = tile("w3_grouped%d" % a, [P, N * PACK], BF16)
+            dst = grouped[:].rearrange("p (c i j) -> p c j i", i=4, j=PACK)
+            src = w3_raw[a][:].rearrange("p j (c i) -> p c j i", i=4)
+            if engine is nc.scalar:
+                nc.scalar.copy(out=dst, in_=src)
+            else:
+                nc.vector.tensor_copy(out=dst, in_=src)
+            return grouped
+
+        picked = {}
+
+        def pick(a, h):
+            picked[a, h] = tile("picked%d%d" % (a, h), [P, HALF], U32)
+            nc.vector.tensor_copy(picked[a, h][:], tab[a][:].indirect(offsets[:, h * 32 : (h + 1) * 32]))
+
+        w2 = tile("w2", [P, 2 * H], U8)
+        nc.vector.tensor_copy(
+            out=w2[:].rearrange("p (b t m e) -> p b m t e", b=2, t=PACK, e=2),
+            in_=w2_raw[:].rearrange("p (b m t e) -> p b m t e", b=2, t=PACK, e=2),
+        )
+        move_rows(w2_plane_raw, w2_rows)
+        w2_plane = tile("w2_plane", [P, H], U8)
+        nc.vector.tensor_copy(
+            out=w2_plane[:].rearrange("p (b t m) -> p b m t", b=2, t=PACK),
+            in_=w2_plane_raw[:].rearrange("p (b m t) -> p b m t", b=2, t=PACK),
+        )
+        picked_plane = tile("picked_plane", [P, S], U8)
+        nc.vector.tensor_copy(picked_plane[:], tab_plane[:].indirect(offsets[:]))
+        for a in range(2):
+            for h in range(2):
+                pick(a, h)
+        w1_q = {}
+        w1_q[0, 0] = quantise("w1_00", round_w1(0, 0, [nc.vector]))
+        w1_q[1, 0] = quantise("w1_10", round_w1(1, 0, [nc.scalar, nc.vector]), pieces=PACK)
+
+        def supply_pass(acc, b, t, h):
+            col = b * PASS + t * P
+            nc.tensor.matmul_mx(
+                out=acc[:],
+                lhsT=w2[:, 2 * col : 2 * (col + P)].bitcast(FP4X4),
+                lhsT_scale=w2_plane[:, col : col + P],
+                rhs=xs[:, h * HALF : (h + 1) * HALF].bitcast(FP8X4),
+                rhs_scale=xs_plane[:, h * HALF : (h + 1) * HALF],
+                start=True, stop=False,
+            )
+
+        def demand_pass(acc, a, b, t, h):
+            codes, plane = w1_q[a, b]
+            nc.tensor.matmul_mx(
+                out=acc[:],
+                lhsT=codes[:, t * P : (t + 1) * P].bitcast(FP8X4),
+                lhsT_scale=plane[:, t * P : (t + 1) * P],
+                rhs=picked[a, h][:].bitcast(FP8X4),
+                rhs_scale=picked_plane[4 * a : P, h * HALF : (h + 1) * HALF],
+                start=False, stop=(a == 1),
+            )
+
+        gap = {}
+
+        def leave_gap(acc, b, t, h):
+            if t == 0:
+                gap[b, h] = tile("gap%d%d" % (b, h), [P, PACK * HALF], BF16)
+            dst = gap[b, h][:, t * HALF : (t + 1) * HALF]
+            nc.scalar.activation(out=dst, in_=acc[:], func=ACT.Identity, scale=-1.0, bias=res[:, b, t : t + 1])
+
+        sides = {}
+
+        def split_gap(b, c0, c1):
+            h = c0 // HALF
+            cols = slice(c0 - h * HALF, c1 - h * HALF)
+            src = gap[b, h][:].rearrange("p (t c) -> p t c", t=PACK)[:, :, cols].rearrange("p t (c i) -> p c t i", i=4)
+            grouped = []
+            for name, op in (("over", ALU.min), ("short", ALU.max)):
+                g = ring.tile([P, (c1 - c0) * PACK], BF16, name=name + "_grouped", align_bytes=64)
+                dst = g[:].rearrange("p (c i t) -> p c t i", i=4, t=PACK)
+                nc.vector.tensor_scalar(out=dst, in0=src, scalar1=0.0, scalar2=None, op0=op)
+                grouped.append(g)
+            over = quantise("over%d_%d" % (b, c0), grouped[0])
+            short = quantise("short%d_%d" % (b, c0), grouped[1])
+            sides[b, c0] = (over, short, c0)
+
+        acc = {}
+        for h in range(2):
+            for t in range(PACK):
+                acc[t, h] = bank(4 * h + t)
+                supply_pass(acc[t, h], 0, t, h)
+        for h in range(2):
+            for t in range(PACK):
+                demand_pass(acc[t, h], 0, 0, t, h)
+            for t in range(PACK):
+                demand_pass(acc[t, h], 1, 0, t, h)
+                leave_gap(acc[t, h], 0, t, h)
+        w1_q[0, 1] = quantise("w1_01", round_w1(0, 1, [nc.vector]))
+        w1_q[1, 1] = quantise("w1_11", round_w1(1, 1, [nc.vector]))
+        for h in range(2):
+            for t in range(PACK):
+                acc[t, h] = bank(4 * h + t)
+                supply_pass(acc[t, h], 1, t, h)
+                demand_pass(acc[t, h], 0, 1, t, h)
+            for t in range(PACK):
+                demand_pass(acc[t, h], 1, 1, t, h)
+                leave_gap(acc[t, h], 1, t, h)
+        split_gap(0, 0, HALF)
+        w3_q = [quantise("w3_0", round_w3(0, nc.scalar))]
+        split_gap(0, HALF, S)
+        split_gap(1, 0, HALF)
+        w3_q.append(quantise("w3_1", round_w3(1, nc.scalar)))
+        chunks = [(0, HALF), (HALF, HALF + HALF // 2), (HALF + HALF // 2, S)]
+        for c0, c1 in chunks[1:]:
+            split_gap(1, c0, c1)
+
+        def score_passes(acc2, a, i, c0, c1):
+            cols = slice(i * P, (i + 1) * P)
+            over, short, first = sides[a, c0] if (a, c0) in sides else sides[a, HALF]
+            tokens = slice(c0 - first, c1 - first)
+            nc.tensor.matmul_mx(
+                out=acc2[:, 0 : c1 - c0],
+                lhsT=w4[:, a, cols].bitcast(FP8X4),
+                lhsT_scale=w4_plane[4 * a : P, cols],
+                rhs=over[0][:, tokens].bitcast(FP8X4),
+                rhs_scale=over[1][:, tokens],
+                start=(a == 0), stop=False,
+            )
+            nc.tensor.matmul_mx(
+                out=acc2[:, 0 : c1 - c0],
+                lhsT=w3_q[a][0][:, cols].bitcast(FP8X4),
+                lhsT_scale=w3_q[a][1][:, cols],
+                rhs=short[0][:, tokens].bitcast(FP8X4),
+                rhs_scale=short[1][:, tokens],
+                start=False, stop=(a == 1),
+            )
+
+        for n, (c0, c1) in enumerate(chunks):
+            scores = [bank(4 * (n % 2) + i) for i in range(N // P)]
+            for i in range(N // P):
+                score_passes(scores[i], 0, i, c0, c1)
+            for i in range(N // P):
+                score_passes(scores[i], 1, i, c0, c1)
+                result = tile("result%d_%d" % (i, c0), [P, c1 - c0], F32)
+                if n == len(chunks) - 1 and i % 2 == 1:
+                    nc.vector.tensor_scalar(out=result[:], in0=scores[i][:, 0 : c1 - c0], scalar1=bias[:, i : i + 1], scalar2=None, op0=ALU.add)
+                else:
+                    nc.scalar.activation(out=result[:], in_=scores[i][:, 0 : c1 - c0], func=ACT.Identity, bias=bias[:, i : i + 1])
+                nc.sync.dma_start(out=out[i * P : (i + 1) * P, c0:c1], in_=result[:])

@@ -75,12 +75,11 @@ def tile_list_fleet_shortage_surplus_kernel(
                 )
             return codes, plane
 
-        xs_plane = zeroed_plane("xs_plane", S)
         tab_plane = zeroed_plane("tab_plane", T)
+        xs_plane = zeroed_plane("xs_plane", S)
         w2_plane_raw = zeroed_plane("w2_plane_raw", H)
         w4_plane = zeroed_plane("w4_plane", N)
         w2_rows = tile("w2_rows", [P, H], U8)
-        load_plane(nc.gpsimd, tab_plane, tab_scales)
 
         w1_raw = {}
         tab = [tile("tab%d" % a, [P, T], U32) for a in range(2)]
@@ -94,15 +93,16 @@ def tile_list_fleet_shortage_surplus_kernel(
         nc.sync.dma_start(out=w2_raw[:].bitcast(I32), in_=w2_words[0].bitcast(I32))
         nc.sync.dma_start(offsets[:], offs)
         load_plane(nc.sync, w2_rows, w2_scales)
-        for a in range(2):
-            nc.sync.dma_start(out=tab[a][:].bitcast(I32), in_=words(tab_words[a]))
+        nc.sync.dma_start(out=tab[0][:].bitcast(I32), in_=words(tab_words[0]))
+        nc.sync.dma_start(out=res[:], in_=reserve.rearrange("(b p t) -> p b t", b=2, t=PACK))
+        load_plane(nc.sync, tab_plane, tab_scales)
+        nc.sync.dma_start(out=tab[1][:].bitcast(I32), in_=words(tab_words[1]))
         load_plane(nc.sync, xs_plane, xs_scales)
         nc.sync.dma_start(out=xs[:].bitcast(I32), in_=words(xs_words[0]))
-        w1_raw[0, 0] = [load_rows("w1_raw00", w1, 0, 0, PASS)]
+        w1_raw[0, 0] = [load_rows("w1_raw00_%d" % u, w1, 0, u * PASS // 2, (u + 1) * PASS // 2) for u in range(2)]
         w1_raw[1, 0] = [load_rows("w1_raw10_%d" % u, w1, 1, u * PASS // 2, (u + 1) * PASS // 2) for u in range(2)]
-        nc.sync.dma_start(out=res[:], in_=reserve.rearrange("(b p t) -> p b t", b=2, t=PACK))
         w1_raw[0, 1] = [load_rows("w1_raw01", w1, 0, PASS, 2 * PASS)]
-        w1_raw[1, 1] = [load_rows("w1_raw11", w1, 1, PASS, 2 * PASS)]
+        w1_raw[1, 1] = [load_rows("w1_raw11_%d" % u, w1, 1, PASS + u * PASS // 2, PASS + (u + 1) * PASS // 2) for u in range(2)]
         w3_raw = [load_rows("w3_raw0", w3, 0, 0, N)]
         load_plane(nc.sync, w4_plane, w4_scales)
         nc.sync.dma_start(out=w4[:].bitcast(I32), in_=w4_words.rearrange("a p c i -> p a (c i)").bitcast(I32))
@@ -155,7 +155,7 @@ def tile_list_fleet_shortage_surplus_kernel(
             for h in range(2):
                 pick(a, h)
         w1_q = {}
-        w1_q[0, 0] = quantise("w1_00", round_w1(0, 0, [nc.vector]))
+        w1_q[0, 0] = quantise("w1_00", round_w1(0, 0, [nc.scalar, nc.vector]), pieces=PACK)
         w1_q[1, 0] = quantise("w1_10", round_w1(1, 0, [nc.scalar, nc.vector]), pieces=PACK)
 
         def supply_pass(acc, b, t, h):
@@ -186,7 +186,10 @@ def tile_list_fleet_shortage_surplus_kernel(
             if t == 0:
                 gap[b, h] = tile("gap%d%d" % (b, h), [P, PACK * HALF], BF16)
             dst = gap[b, h][:, t * HALF : (t + 1) * HALF]
-            nc.scalar.activation(out=dst, in_=acc[:], func=ACT.Identity, scale=-1.0, bias=res[:, b, t : t + 1])
+            if (b, h) == (0, 0) and t >= 2:
+                nc.vector.tensor_scalar(out=dst, in0=acc[:], scalar1=-1.0, scalar2=res[:, b, t : t + 1], op0=ALU.mult, op1=ALU.add)
+            else:
+                nc.scalar.activation(out=dst, in_=acc[:], func=ACT.Identity, scale=-1.0, bias=res[:, b, t : t + 1])
 
         sides = {}
 
@@ -216,7 +219,7 @@ def tile_list_fleet_shortage_surplus_kernel(
                 demand_pass(acc[t, h], 1, 0, t, h)
                 leave_gap(acc[t, h], 0, t, h)
         w1_q[0, 1] = quantise("w1_01", round_w1(0, 1, [nc.vector]))
-        w1_q[1, 1] = quantise("w1_11", round_w1(1, 1, [nc.vector]))
+        w1_q[1, 1] = quantise("w1_11", round_w1(1, 1, [nc.scalar, nc.vector]))
         for h in range(2):
             for t in range(PACK):
                 acc[t, h] = bank(4 * h + t)

@@ -29,7 +29,7 @@ def tile_list_fleet_shortage_surplus_kernel(
     nc = tc.nc
     with ExitStack() as ctx:
         keep = ctx.enter_context(tc.tile_pool(name="keep", bufs=1))
-        ring = ctx.enter_context(tc.tile_pool(name="ring", bufs=2))
+        ring = ctx.enter_context(tc.tile_pool(name="ring", bufs=1))
         psum = ctx.enter_context(tc.psum_pool(name="psum", bufs=1))
 
         def tile(name, shape, dtype):
@@ -49,8 +49,10 @@ def tile_list_fleet_shortage_surplus_kernel(
         def load_plane(queue, plane, scales):
             passes = scales.shape[0]
             for q in range(4):
-                src = scales[:, 4 * q : 4 * q + 4, :] if passes > 1 else scales[0, 4 * q : 4 * q + 4, :]
-                queue.dma_start(out=plane[32 * q : 32 * q + 4 * passes, :].bitcast(I32), in_=src.bitcast(I32))
+                if passes > 1:
+                    queue.dma_start(out=plane[32 * q : 32 * q + 4 * passes, :].bitcast(I32), in_=scales[:, 4 * q : 4 * q + 4, :].bitcast(I32))
+                else:
+                    queue.dma_start(out=plane[q:P:32, :].bitcast(I32), in_=scales[0, q:16:4, :].bitcast(I32))
 
         def move_rows(plane, rows, passes=1):
             for q in range(4):
@@ -94,15 +96,15 @@ def tile_list_fleet_shortage_surplus_kernel(
         nc.sync.dma_start(offsets[:], offs)
         load_plane(nc.sync, w2_rows, w2_scales)
         nc.sync.dma_start(out=tab[0][:].bitcast(I32), in_=words(tab_words[0]))
-        nc.sync.dma_start(out=res[:], in_=reserve.rearrange("(b p t) -> p b t", b=2, t=PACK))
+        nc.sync.dma_start(out=xs[:].bitcast(I32), in_=words(xs_words[0]))
         load_plane(nc.sync, tab_plane, tab_scales)
         nc.sync.dma_start(out=tab[1][:].bitcast(I32), in_=words(tab_words[1]))
         load_plane(nc.sync, xs_plane, xs_scales)
-        nc.sync.dma_start(out=xs[:].bitcast(I32), in_=words(xs_words[0]))
-        w1_raw[0, 0] = [load_rows("w1_raw00_%d" % u, w1, 0, u * PASS // 2, (u + 1) * PASS // 2) for u in range(2)]
+        w1_raw[0, 0] = [load_rows("w1_raw00", w1, 0, 0, PASS)]
         w1_raw[1, 0] = [load_rows("w1_raw10_%d" % u, w1, 1, u * PASS // 2, (u + 1) * PASS // 2) for u in range(2)]
+        nc.sync.dma_start(out=res[:], in_=reserve.rearrange("(b p t) -> p b t", b=2, t=PACK))
         w1_raw[0, 1] = [load_rows("w1_raw01", w1, 0, PASS, 2 * PASS)]
-        w1_raw[1, 1] = [load_rows("w1_raw11_%d" % u, w1, 1, PASS + u * PASS // 2, PASS + (u + 1) * PASS // 2) for u in range(2)]
+        w1_raw[1, 1] = [load_rows("w1_raw11", w1, 1, PASS, 2 * PASS)]
         w3_raw = [load_rows("w3_raw0", w3, 0, 0, N)]
         load_plane(nc.sync, w4_plane, w4_scales)
         nc.sync.dma_start(out=w4[:].bitcast(I32), in_=w4_words.rearrange("a p c i -> p a (c i)").bitcast(I32))
@@ -111,7 +113,10 @@ def tile_list_fleet_shortage_surplus_kernel(
             nc.sync.dma_start(out=bias[:], in_=base.rearrange("(i p) -> p i", p=P))
 
         def round_w1(a, b, engines):
-            grouped = tile("w1_grouped%d%d" % (a, b), [P, PASS * PACK], BF16)
+            if (a, b) == (1, 1):
+                grouped = ring.tile([P, PASS * PACK], BF16, name="over_grouped", align_bytes=64)
+            else:
+                grouped = tile("w1_grouped%d%d" % (a, b), [P, PASS * PACK], BF16)
             share = P // len(engines)
             for u, engine in enumerate(engines):
                 dst = grouped[:].rearrange("p (t m j) -> p m j t", t=PACK, j=PACK)[:, u * share : (u + 1) * share]
@@ -155,7 +160,7 @@ def tile_list_fleet_shortage_surplus_kernel(
             for h in range(2):
                 pick(a, h)
         w1_q = {}
-        w1_q[0, 0] = quantise("w1_00", round_w1(0, 0, [nc.scalar, nc.vector]), pieces=PACK)
+        w1_q[0, 0] = quantise("w1_00", round_w1(0, 0, [nc.vector]), pieces=PACK)
         w1_q[1, 0] = quantise("w1_10", round_w1(1, 0, [nc.scalar, nc.vector]), pieces=PACK)
 
         def supply_pass(acc, b, t, h):
@@ -185,7 +190,7 @@ def tile_list_fleet_shortage_surplus_kernel(
         def leave_gap(acc, b, t, h):
             if t == 0:
                 gap[b, h] = tile("gap%d%d" % (b, h), [P, PACK * HALF], BF16)
-            dst = gap[b, h][:, t * HALF : (t + 1) * HALF]
+            dst = gap[b, h][:].rearrange("p (u c e) -> p u e c", u=2, e=2)[:, t // 2, t % 2, :]
             if (b, h) == (0, 0) and t >= 2:
                 nc.vector.tensor_scalar(out=dst, in0=acc[:], scalar1=-1.0, scalar2=res[:, b, t : t + 1], op0=ALU.mult, op1=ALU.add)
             else:
@@ -196,11 +201,11 @@ def tile_list_fleet_shortage_surplus_kernel(
         def split_gap(b, c0, c1):
             h = c0 // HALF
             cols = slice(c0 - h * HALF, c1 - h * HALF)
-            src = gap[b, h][:].rearrange("p (t c) -> p t c", t=PACK)[:, :, cols].rearrange("p t (c i) -> p c t i", i=4)
+            src = gap[b, h][:].rearrange("p (u c e) -> p c u e", u=2, e=2)[:, cols]
             grouped = []
             for name, op in (("over", ALU.min), ("short", ALU.max)):
                 g = ring.tile([P, (c1 - c0) * PACK], BF16, name=name + "_grouped", align_bytes=64)
-                dst = g[:].rearrange("p (c i t) -> p c t i", i=4, t=PACK)
+                dst = g[:].rearrange("p (c u e) -> p c u e", u=2, e=2)
                 nc.vector.tensor_scalar(out=dst, in0=src, scalar1=0.0, scalar2=None, op0=op)
                 grouped.append(g)
             over = quantise("over%d_%d" % (b, c0), grouped[0])
@@ -219,7 +224,7 @@ def tile_list_fleet_shortage_surplus_kernel(
                 demand_pass(acc[t, h], 1, 0, t, h)
                 leave_gap(acc[t, h], 0, t, h)
         w1_q[0, 1] = quantise("w1_01", round_w1(0, 1, [nc.vector]))
-        w1_q[1, 1] = quantise("w1_11", round_w1(1, 1, [nc.scalar, nc.vector]))
+        w1_q[1, 1] = quantise("w1_11", round_w1(1, 1, [nc.vector]), pieces=PACK)
         for h in range(2):
             for t in range(PACK):
                 acc[t, h] = bank(4 * h + t)
@@ -229,10 +234,10 @@ def tile_list_fleet_shortage_surplus_kernel(
                 demand_pass(acc[t, h], 1, 1, t, h)
                 leave_gap(acc[t, h], 1, t, h)
         split_gap(0, 0, HALF)
-        w3_q = [quantise("w3_0", round_w3(0, nc.scalar))]
+        w3_q = [quantise("w3_0", round_w3(0, nc.vector))]
         split_gap(0, HALF, S)
         split_gap(1, 0, HALF)
-        w3_q.append(quantise("w3_1", round_w3(1, nc.scalar)))
+        w3_q.append(quantise("w3_1", round_w3(1, nc.vector)))
         chunks = [(0, HALF), (HALF, HALF + HALF // 2), (HALF + HALF // 2, S)]
         for c0, c1 in chunks[1:]:
             split_gap(1, c0, c1)

@@ -20,6 +20,9 @@ P = 128
 PACK = 4
 PASS = P * PACK
 HALF = 512
+QUADS = 4
+LIST_COLS = HALF // 16
+ALIGN = 256
 
 
 def tile_list_fleet_shortage_surplus_kernel(
@@ -33,7 +36,7 @@ def tile_list_fleet_shortage_surplus_kernel(
         psum = ctx.enter_context(tc.psum_pool(name="psum", bufs=1))
 
         def tile(name, shape, dtype):
-            return keep.tile(shape, dtype, name=name, align_bytes=64)
+            return keep.tile(shape, dtype, name=name, align_bytes=ALIGN)
 
         def bank(i):
             return psum.tile([P, HALF], F32, name="bank%d" % i)
@@ -46,18 +49,14 @@ def tile_list_fleet_shortage_surplus_kernel(
             nc.vector.memset(plane[:].bitcast(I32), 0)
             return plane
 
-        def load_plane(queue, plane, scales):
+        def load_plane(plane, scales):
             passes = scales.shape[0]
-            for q in range(4):
+            for q in range(QUADS):
                 if passes > 1:
-                    queue.dma_start(out=plane[32 * q : 32 * q + 4 * passes, :].bitcast(I32), in_=scales[:, 4 * q : 4 * q + 4, :].bitcast(I32))
+                    dst, src = plane[32 * q : 32 * q + 4 * passes, :], scales[:, 4 * q : 4 * q + 4, :]
                 else:
-                    queue.dma_start(out=plane[q:P:32, :].bitcast(I32), in_=scales[0, q:16:4, :].bitcast(I32))
-
-        def move_rows(plane, rows, passes=1):
-            for q in range(4):
-                live = slice(32 * q, 32 * q + 4 * passes)
-                nc.vector.tensor_copy(out=plane[live, :].bitcast(I32), in_=rows[live, :].bitcast(I32))
+                    dst, src = plane[q:P:32, :], scales[0, q:16:4, :]
+                nc.sync.dma_start(out=dst.bitcast(I32), in_=src.bitcast(I32))
 
         def load_rows(name, w, a, c0, c1):
             raw = tile(name, [P, PACK, c1 - c0], F32)
@@ -94,29 +93,25 @@ def tile_list_fleet_shortage_surplus_kernel(
 
         nc.sync.dma_start(out=w2_raw[:].bitcast(I32), in_=w2_words[0].bitcast(I32))
         nc.sync.dma_start(offsets[:], offs)
-        load_plane(nc.sync, w2_rows, w2_scales)
+        load_plane(w2_rows, w2_scales)
         nc.sync.dma_start(out=tab[0][:].bitcast(I32), in_=words(tab_words[0]))
         nc.sync.dma_start(out=xs[:].bitcast(I32), in_=words(xs_words[0]))
-        load_plane(nc.sync, tab_plane, tab_scales)
+        load_plane(tab_plane, tab_scales)
         nc.sync.dma_start(out=tab[1][:].bitcast(I32), in_=words(tab_words[1]))
-        load_plane(nc.sync, xs_plane, xs_scales)
+        load_plane(xs_plane, xs_scales)
         w1_raw[0, 0] = [load_rows("w1_raw00", w1, 0, 0, PASS)]
         w1_raw[1, 0] = [load_rows("w1_raw10_%d" % u, w1, 1, u * PASS // 2, (u + 1) * PASS // 2) for u in range(2)]
         nc.sync.dma_start(out=res[:], in_=reserve.rearrange("(b p t) -> p b t", b=2, t=PACK))
         w1_raw[0, 1] = [load_rows("w1_raw01", w1, 0, PASS, 2 * PASS)]
         w1_raw[1, 1] = [load_rows("w1_raw11", w1, 1, PASS, 2 * PASS)]
         w3_raw = [load_rows("w3_raw0", w3, 0, 0, N)]
-        load_plane(nc.sync, w4_plane, w4_scales)
+        load_plane(w4_plane, w4_scales)
         nc.sync.dma_start(out=w4[:].bitcast(I32), in_=w4_words.rearrange("a p c i -> p a (c i)").bitcast(I32))
         w3_raw.append(load_rows("w3_raw1", w3, 1, 0, N))
         with nc.allow_non_contiguous_dma(reason="one value of base to a partition"):
             nc.sync.dma_start(out=bias[:], in_=base.rearrange("(i p) -> p i", p=P))
 
-        def round_w1(a, b, engines):
-            if (a, b) == (1, 1):
-                grouped = ring.tile([P, PASS * PACK], BF16, name="over_grouped", align_bytes=64)
-            else:
-                grouped = tile("w1_grouped%d%d" % (a, b), [P, PASS * PACK], BF16)
+        def round_w1(a, b, engines, grouped):
             share = P // len(engines)
             for u, engine in enumerate(engines):
                 dst = grouped[:].rearrange("p (t m j) -> p m j t", t=PACK, j=PACK)[:, u * share : (u + 1) * share]
@@ -127,46 +122,42 @@ def tile_list_fleet_shortage_surplus_kernel(
                     nc.vector.tensor_scalar(out=dst, in0=src, scalar1=-1.0, scalar2=None, op0=ALU.mult)
             return grouped
 
-        def round_w3(a, engine):
-            grouped = tile("w3_grouped%d" % a, [P, N * PACK], BF16)
-            dst = grouped[:].rearrange("p (c i j) -> p c j i", i=4, j=PACK)
-            src = w3_raw[a][:].rearrange("p j (c i) -> p c j i", i=4)
-            if engine is nc.scalar:
-                nc.scalar.copy(out=dst, in_=src)
-            else:
-                nc.vector.tensor_copy(out=dst, in_=src)
-            return grouped
+        def w1_tile(a, b):
+            return tile("w1_grouped%d%d" % (a, b), [P, PASS * PACK], BF16)
 
-        picked = {}
-
-        def pick(a, h):
-            picked[a, h] = tile("picked%d%d" % (a, h), [P, HALF], U32)
-            nc.vector.tensor_copy(picked[a, h][:], tab[a][:].indirect(offsets[:, h * 32 : (h + 1) * 32]))
+        def side_tile(name, entries):
+            return ring.tile([P, entries * PACK], BF16, name=name + "_grouped", align_bytes=ALIGN)
 
         w2 = tile("w2", [P, 2 * H], U8)
         nc.vector.tensor_copy(
-            out=w2[:].rearrange("p (b t m e) -> p b m t e", b=2, t=PACK, e=2),
-            in_=w2_raw[:].rearrange("p (b m t e) -> p b m t e", b=2, t=PACK, e=2),
+            out=w2[:].rearrange("p (b t m e) -> p b t m e", b=2, t=PACK, e=2),
+            in_=w2_raw[:].rearrange("p (b m t e) -> p b t m e", b=2, t=PACK, e=2),
         )
-        move_rows(w2_plane_raw, w2_rows)
+        for q in range(QUADS):
+            live = slice(32 * q, 32 * q + 4)
+            nc.vector.tensor_copy(out=w2_plane_raw[live, :].bitcast(I32), in_=w2_rows[live, :].bitcast(I32))
         w2_plane = tile("w2_plane", [P, H], U8)
         nc.vector.tensor_copy(
-            out=w2_plane[:].rearrange("p (b t m) -> p b m t", b=2, t=PACK),
-            in_=w2_plane_raw[:].rearrange("p (b m t) -> p b m t", b=2, t=PACK),
+            out=w2_plane[:].rearrange("p (b t m) -> p b t m", b=2, t=PACK),
+            in_=w2_plane_raw[:].rearrange("p (b m t) -> p b t m", b=2, t=PACK),
         )
+
         picked_plane = tile("picked_plane", [P, S], U8)
         nc.vector.tensor_copy(picked_plane[:], tab_plane[:].indirect(offsets[:]))
+        picked = {}
         for a in range(2):
             for h in range(2):
-                pick(a, h)
+                picked[a, h] = tile("picked%d%d" % (a, h), [P, HALF], U32)
+                entries = offsets[:, h * LIST_COLS : (h + 1) * LIST_COLS]
+                nc.vector.tensor_copy(picked[a, h][:], tab[a][:].indirect(entries))
         w1_q = {}
-        w1_q[0, 0] = quantise("w1_00", round_w1(0, 0, [nc.vector]), pieces=PACK)
-        w1_q[1, 0] = quantise("w1_10", round_w1(1, 0, [nc.scalar, nc.vector]), pieces=PACK)
+        w1_q[0, 0] = quantise("w1_00", round_w1(0, 0, [nc.vector], w1_tile(0, 0)), pieces=PACK)
+        w1_q[1, 0] = quantise("w1_10", round_w1(1, 0, [nc.scalar, nc.vector], w1_tile(1, 0)), pieces=PACK)
 
-        def supply_pass(acc, b, t, h):
+        def supply_pass(group, b, t, h):
             col = b * PASS + t * P
             nc.tensor.matmul_mx(
-                out=acc[:],
+                out=group[:],
                 lhsT=w2[:, 2 * col : 2 * (col + P)].bitcast(FP4X4),
                 lhsT_scale=w2_plane[:, col : col + P],
                 rhs=xs[:, h * HALF : (h + 1) * HALF].bitcast(FP8X4),
@@ -174,10 +165,10 @@ def tile_list_fleet_shortage_surplus_kernel(
                 start=True, stop=False,
             )
 
-        def demand_pass(acc, a, b, t, h):
+        def demand_pass(group, a, b, t, h):
             codes, plane = w1_q[a, b]
             nc.tensor.matmul_mx(
-                out=acc[:],
+                out=group[:],
                 lhsT=codes[:, t * P : (t + 1) * P].bitcast(FP8X4),
                 lhsT_scale=plane[:, t * P : (t + 1) * P],
                 rhs=picked[a, h][:].bitcast(FP8X4),
@@ -187,87 +178,98 @@ def tile_list_fleet_shortage_surplus_kernel(
 
         gap = {}
 
-        def leave_gap(acc, b, t, h):
+        def leave_gap(group, b, t, h):
             if t == 0:
                 gap[b, h] = tile("gap%d%d" % (b, h), [P, PACK * HALF], BF16)
             dst = gap[b, h][:].rearrange("p (u c e) -> p u e c", u=2, e=2)[:, t // 2, t % 2, :]
-            if (b, h) == (0, 0) and t >= 2:
-                nc.vector.tensor_scalar(out=dst, in0=acc[:], scalar1=-1.0, scalar2=res[:, b, t : t + 1], op0=ALU.mult, op1=ALU.add)
+            if (b, h) == (0, 0) and t // 2 == 1:
+                nc.vector.tensor_scalar(out=dst, in0=group[:], scalar1=-1.0, scalar2=res[:, b, t : t + 1], op0=ALU.mult, op1=ALU.add)
             else:
-                nc.scalar.activation(out=dst, in_=acc[:], func=ACT.Identity, scale=-1.0, bias=res[:, b, t : t + 1])
+                nc.scalar.activation(out=dst, in_=group[:], func=ACT.Identity, scale=-1.0, bias=res[:, b, t : t + 1])
 
         sides = {}
 
         def split_gap(b, c0, c1):
             h = c0 // HALF
-            cols = slice(c0 - h * HALF, c1 - h * HALF)
-            src = gap[b, h][:].rearrange("p (u c e) -> p c u e", u=2, e=2)[:, cols]
+            src = gap[b, h][:].rearrange("p (u c e) -> p c u e", u=2, e=2)[:, c0 - h * HALF : c1 - h * HALF]
             grouped = []
             for name, op in (("over", ALU.min), ("short", ALU.max)):
-                g = ring.tile([P, (c1 - c0) * PACK], BF16, name=name + "_grouped", align_bytes=64)
-                dst = g[:].rearrange("p (c u e) -> p c u e", u=2, e=2)
+                side = side_tile(name, c1 - c0)
+                dst = side[:].rearrange("p (c u e) -> p c u e", u=2, e=2)
                 nc.vector.tensor_scalar(out=dst, in0=src, scalar1=0.0, scalar2=None, op0=op)
-                grouped.append(g)
+                grouped.append(side)
             over = quantise("over%d_%d" % (b, c0), grouped[0])
             short = quantise("short%d_%d" % (b, c0), grouped[1])
-            sides[b, c0] = (over, short, c0)
+            sides[b, c0] = (over, short)
 
-        acc = {}
+        def quantise_w3(a):
+            grouped = tile("w3_grouped%d" % a, [P, N * PACK], BF16)
+            nc.vector.tensor_copy(
+                out=grouped[:].rearrange("p (c i j) -> p c j i", i=4, j=PACK),
+                in_=w3_raw[a][:].rearrange("p j (c i) -> p c j i", i=4),
+            )
+            return quantise("w3_%d" % a, grouped)
+
+        groups = {}
         for h in range(2):
             for t in range(PACK):
-                acc[t, h] = bank(4 * h + t)
-                supply_pass(acc[t, h], 0, t, h)
+                groups[t, h] = bank(PACK * h + t)
+                supply_pass(groups[t, h], 0, t, h)
         for h in range(2):
             for t in range(PACK):
-                demand_pass(acc[t, h], 0, 0, t, h)
+                demand_pass(groups[t, h], 0, 0, t, h)
             for t in range(PACK):
-                demand_pass(acc[t, h], 1, 0, t, h)
-                leave_gap(acc[t, h], 0, t, h)
-        w1_q[0, 1] = quantise("w1_01", round_w1(0, 1, [nc.vector]))
-        w1_q[1, 1] = quantise("w1_11", round_w1(1, 1, [nc.vector]), pieces=PACK)
+                demand_pass(groups[t, h], 1, 0, t, h)
+                leave_gap(groups[t, h], 0, t, h)
+        w1_q[0, 1] = quantise("w1_01", round_w1(0, 1, [nc.vector], w1_tile(0, 1)))
+        w1_q[1, 1] = quantise("w1_11", round_w1(1, 1, [nc.vector], side_tile("over", PASS)), pieces=PACK)
         for h in range(2):
             for t in range(PACK):
-                acc[t, h] = bank(4 * h + t)
-                supply_pass(acc[t, h], 1, t, h)
-                demand_pass(acc[t, h], 0, 1, t, h)
+                groups[t, h] = bank(PACK * h + t)
+                supply_pass(groups[t, h], 1, t, h)
+                demand_pass(groups[t, h], 0, 1, t, h)
             for t in range(PACK):
-                demand_pass(acc[t, h], 1, 1, t, h)
-                leave_gap(acc[t, h], 1, t, h)
+                demand_pass(groups[t, h], 1, 1, t, h)
+                leave_gap(groups[t, h], 1, t, h)
+
+        chunks = [(0, HALF), (HALF, HALF + HALF // 2), (HALF + HALF // 2, S)]
         split_gap(0, 0, HALF)
-        w3_q = [quantise("w3_0", round_w3(0, nc.vector))]
+        w3_q = [quantise_w3(0)]
         split_gap(0, HALF, S)
         split_gap(1, 0, HALF)
-        w3_q.append(quantise("w3_1", round_w3(1, nc.vector)))
-        chunks = [(0, HALF), (HALF, HALF + HALF // 2), (HALF + HALF // 2, S)]
+        w3_q.append(quantise_w3(1))
         for c0, c1 in chunks[1:]:
             split_gap(1, c0, c1)
 
-        def score_passes(acc2, a, i, c0, c1):
+        def score_passes(group, b, i, c0, c1):
             cols = slice(i * P, (i + 1) * P)
-            over, short, first = sides[a, c0] if (a, c0) in sides else sides[a, HALF]
-            tokens = slice(c0 - first, c1 - first)
+            first = c0 if b == 1 else c0 // HALF * HALF
+            (over_codes, over_plane), (short_codes, short_plane) = sides[b, first]
+            w3_codes, w3_plane = w3_q[b]
+            entries = slice(c0 - first, c1 - first)
             nc.tensor.matmul_mx(
-                out=acc2[:, 0 : c1 - c0],
-                lhsT=w4[:, a, cols].bitcast(FP8X4),
-                lhsT_scale=w4_plane[4 * a : P, cols],
-                rhs=over[0][:, tokens].bitcast(FP8X4),
-                rhs_scale=over[1][:, tokens],
-                start=(a == 0), stop=False,
+                out=group[:, 0 : c1 - c0],
+                lhsT=w4[:, b, cols].bitcast(FP8X4),
+                lhsT_scale=w4_plane[4 * b : P, cols],
+                rhs=over_codes[:, entries].bitcast(FP8X4),
+                rhs_scale=over_plane[:, entries],
+                start=(b == 0), stop=False,
             )
             nc.tensor.matmul_mx(
-                out=acc2[:, 0 : c1 - c0],
-                lhsT=w3_q[a][0][:, cols].bitcast(FP8X4),
-                lhsT_scale=w3_q[a][1][:, cols],
-                rhs=short[0][:, tokens].bitcast(FP8X4),
-                rhs_scale=short[1][:, tokens],
-                start=False, stop=(a == 1),
+                out=group[:, 0 : c1 - c0],
+                lhsT=w3_codes[:, cols].bitcast(FP8X4),
+                lhsT_scale=w3_plane[:, cols],
+                rhs=short_codes[:, entries].bitcast(FP8X4),
+                rhs_scale=short_plane[:, entries],
+                start=False, stop=(b == 1),
             )
 
+        row_tiles = N // P
         for n, (c0, c1) in enumerate(chunks):
-            scores = [bank(4 * (n % 2) + i) for i in range(N // P)]
-            for i in range(N // P):
+            scores = [bank(row_tiles * (n % 2) + i) for i in range(row_tiles)]
+            for i in range(row_tiles):
                 score_passes(scores[i], 0, i, c0, c1)
-            for i in range(N // P):
+            for i in range(row_tiles):
                 score_passes(scores[i], 1, i, c0, c1)
                 result = tile("result%d_%d" % (i, c0), [P, c1 - c0], F32)
                 if n == len(chunks) - 1 and i % 2 == 1:

from contextlib import ExitStack

import concourse.mybir as mybir

K, T, S, K2, H, N = 1024, 4096, 1024, 512, 1024, 512
FLOPS = 2 * S * (K * H + K2 * H + 2 * H * N)

F32 = mybir.dt.float32
BF16 = mybir.dt.bfloat16
I32 = mybir.dt.int32
U32 = mybir.dt.uint32
U16 = mybir.dt.uint16
U8 = mybir.dt.uint8
FP8X4 = mybir.dt.float8_e4m3fn_x4
FP4X4 = mybir.dt.float4_e2m1fn_x4
ALU = mybir.AluOpType
ACT = mybir.ActivationFunctionType

P = 128
PACK = 4
PASS = P * PACK
HALF = 512
QUADS = 4
LIST_COLS = HALF // 16
ALIGN = 256


def tile_list_fleet_shortage_surplus_kernel(
    tc, tab_words, tab_scales, offs, xs_words, xs_scales, w1, w2_words, w2_scales,
    reserve, w3, w4_words, w4_scales, base, out,
):
    nc = tc.nc
    with ExitStack() as ctx:
        keep = ctx.enter_context(tc.tile_pool(name="keep", bufs=1))
        ring = ctx.enter_context(tc.tile_pool(name="ring", bufs=1))
        psum = ctx.enter_context(tc.psum_pool(name="psum", bufs=1))

        def tile(name, shape, dtype):
            return keep.tile(shape, dtype, name=name, align_bytes=ALIGN)

        def bank(i):
            return psum.tile([P, HALF], F32, name="bank%d" % i)

        def words(ap):
            return ap.rearrange("p c i -> p (c i)").bitcast(I32)

        def zeroed_plane(name, width):
            plane = tile(name, [P, width], U8)
            nc.vector.memset(plane[:].bitcast(I32), 0)
            return plane

        def load_plane(plane, scales):
            passes = scales.shape[0]
            for q in range(QUADS):
                if passes > 1:
                    dst, src = plane[32 * q : 32 * q + 4 * passes, :], scales[:, 4 * q : 4 * q + 4, :]
                else:
                    dst, src = plane[q:P:32, :], scales[0, q:16:4, :]
                nc.sync.dma_start(out=dst.bitcast(I32), in_=src.bitcast(I32))

        def load_rows(name, w, a, c0, c1):
            raw = tile(name, [P, PACK, c1 - c0], F32)
            nc.sync.dma_start(out=raw[:], in_=w[a * PASS : (a + 1) * PASS, c0:c1].rearrange("(p j) c -> p j c", j=PACK))
            return raw

        def quantise(name, grouped, pieces=1):
            width = grouped.shape[1] // PACK
            codes = tile(name + "_codes", [P, width], U32)
            plane = tile(name + "_plane", [P, width], U8)
            step = width // pieces
            for c in range(0, width, step):
                nc.vector.quantize_mx(
                    out=codes[:, c : c + step].bitcast(FP8X4),
                    scales=plane[:, c : c + step],
                    in_=grouped[:, PACK * c : PACK * (c + step)],
                )
            return codes, plane

        tab_plane = zeroed_plane("tab_plane", T)
        xs_plane = zeroed_plane("xs_plane", S)
        w2_plane_raw = zeroed_plane("w2_plane_raw", H)
        w4_plane = zeroed_plane("w4_plane", N)
        w2_rows = tile("w2_rows", [P, H], U8)

        w1_raw = {}
        tab = [tile("tab%d" % a, [P, T], U32) for a in range(2)]
        offsets = keep.tile([P, S // 16], U16, name="offsets")
        w2_raw = tile("w2_raw", [P, 2 * H], U8)
        xs = tile("xs", [P, S], U32)
        res = tile("res", [P, 2, PACK], F32)
        w4 = tile("w4", [P, 2, N], U32)
        bias = tile("bias", [P, N // P], F32)

        nc.sync.dma_start(out=w2_raw[:].bitcast(I32), in_=w2_words[0].bitcast(I32))
        nc.sync.dma_start(offsets[:], offs)
        load_plane(w2_rows, w2_scales)
        nc.sync.dma_start(out=tab[0][:].bitcast(I32), in_=words(tab_words[0]))
        nc.sync.dma_start(out=xs[:].bitcast(I32), in_=words(xs_words[0]))
        load_plane(tab_plane, tab_scales)
        nc.sync.dma_start(out=tab[1][:].bitcast(I32), in_=words(tab_words[1]))
        load_plane(xs_plane, xs_scales)
        w1_raw[0, 0] = [load_rows("w1_raw00", w1, 0, 0, PASS)]
        w1_raw[1, 0] = [load_rows("w1_raw10_%d" % u, w1, 1, u * PASS // 2, (u + 1) * PASS // 2) for u in range(2)]
        nc.sync.dma_start(out=res[:], in_=reserve.rearrange("(b p t) -> p b t", b=2, t=PACK))
        w1_raw[0, 1] = [load_rows("w1_raw01", w1, 0, PASS, 2 * PASS)]
        w1_raw[1, 1] = [load_rows("w1_raw11", w1, 1, PASS, 2 * PASS)]
        w3_raw = [load_rows("w3_raw0", w3, 0, 0, N)]
        load_plane(w4_plane, w4_scales)
        nc.sync.dma_start(out=w4[:].bitcast(I32), in_=w4_words.rearrange("a p c i -> p a (c i)").bitcast(I32))
        w3_raw.append(load_rows("w3_raw1", w3, 1, 0, N))
        with nc.allow_non_contiguous_dma(reason="one value of base to a partition"):
            nc.sync.dma_start(out=bias[:], in_=base.rearrange("(i p) -> p i", p=P))

        def round_w1(a, b, engines, grouped):
            share = P // len(engines)
            for u, engine in enumerate(engines):
                dst = grouped[:].rearrange("p (t m j) -> p m j t", t=PACK, j=PACK)[:, u * share : (u + 1) * share]
                src = w1_raw[a, b][u][:].rearrange("p j (m t) -> p m j t", t=PACK)
                if engine is nc.scalar:
                    nc.scalar.activation(out=dst, in_=src, func=ACT.Copy, scale=-1.0)
                else:
                    nc.vector.tensor_scalar(out=dst, in0=src, scalar1=-1.0, scalar2=None, op0=ALU.mult)
            return grouped

        def w1_tile(a, b):
            return tile("w1_grouped%d%d" % (a, b), [P, PASS * PACK], BF16)

        def side_tile(name, entries):
            return ring.tile([P, entries * PACK], BF16, name=name + "_grouped", align_bytes=ALIGN)

        w2 = tile("w2", [P, 2 * H], U8)
        nc.vector.tensor_copy(
            out=w2[:].rearrange("p (b t m e) -> p b t m e", b=2, t=PACK, e=2),
            in_=w2_raw[:].rearrange("p (b m t e) -> p b t m e", b=2, t=PACK, e=2),
        )
        for q in range(QUADS):
            live = slice(32 * q, 32 * q + 4)
            nc.vector.tensor_copy(out=w2_plane_raw[live, :].bitcast(I32), in_=w2_rows[live, :].bitcast(I32))
        w2_plane = tile("w2_plane", [P, H], U8)
        nc.vector.tensor_copy(
            out=w2_plane[:].rearrange("p (b t m) -> p b t m", b=2, t=PACK),
            in_=w2_plane_raw[:].rearrange("p (b m t) -> p b t m", b=2, t=PACK),
        )

        picked_plane = tile("picked_plane", [P, S], U8)
        nc.vector.tensor_copy(picked_plane[:], tab_plane[:].indirect(offsets[:]))
        picked = {}
        for a in range(2):
            for h in range(2):
                picked[a, h] = tile("picked%d%d" % (a, h), [P, HALF], U32)
                entries = offsets[:, h * LIST_COLS : (h + 1) * LIST_COLS]
                nc.vector.tensor_copy(picked[a, h][:], tab[a][:].indirect(entries))
        w1_q = {}
        w1_q[0, 0] = quantise("w1_00", round_w1(0, 0, [nc.vector], w1_tile(0, 0)), pieces=PACK)
        w1_q[1, 0] = quantise("w1_10", round_w1(1, 0, [nc.scalar, nc.vector], w1_tile(1, 0)), pieces=PACK)

        def supply_pass(group, b, t, h):
            col = b * PASS + t * P
            nc.tensor.matmul_mx(
                out=group[:],
                lhsT=w2[:, 2 * col : 2 * (col + P)].bitcast(FP4X4),
                lhsT_scale=w2_plane[:, col : col + P],
                rhs=xs[:, h * HALF : (h + 1) * HALF].bitcast(FP8X4),
                rhs_scale=xs_plane[:, h * HALF : (h + 1) * HALF],
                start=True, stop=False,
            )

        def demand_pass(group, a, b, t, h):
            codes, plane = w1_q[a, b]
            nc.tensor.matmul_mx(
                out=group[:],
                lhsT=codes[:, t * P : (t + 1) * P].bitcast(FP8X4),
                lhsT_scale=plane[:, t * P : (t + 1) * P],
                rhs=picked[a, h][:].bitcast(FP8X4),
                rhs_scale=picked_plane[4 * a : P, h * HALF : (h + 1) * HALF],
                start=False, stop=(a == 1),
            )

        gap = {}

        def leave_gap(group, b, t, h):
            if t == 0:
                gap[b, h] = tile("gap%d%d" % (b, h), [P, PACK * HALF], BF16)
            dst = gap[b, h][:].rearrange("p (u c e) -> p u e c", u=2, e=2)[:, t // 2, t % 2, :]
            if (b, h) == (0, 0) and t // 2 == 1:
                nc.vector.tensor_scalar(out=dst, in0=group[:], scalar1=-1.0, scalar2=res[:, b, t : t + 1], op0=ALU.mult, op1=ALU.add)
            else:
                nc.scalar.activation(out=dst, in_=group[:], func=ACT.Identity, scale=-1.0, bias=res[:, b, t : t + 1])

        sides = {}

        def split_gap(b, c0, c1):
            h = c0 // HALF
            src = gap[b, h][:].rearrange("p (u c e) -> p c u e", u=2, e=2)[:, c0 - h * HALF : c1 - h * HALF]
            grouped = []
            for name, op in (("over", ALU.min), ("short", ALU.max)):
                side = side_tile(name, c1 - c0)
                dst = side[:].rearrange("p (c u e) -> p c u e", u=2, e=2)
                nc.vector.tensor_scalar(out=dst, in0=src, scalar1=0.0, scalar2=None, op0=op)
                grouped.append(side)
            over = quantise("over%d_%d" % (b, c0), grouped[0])
            short = quantise("short%d_%d" % (b, c0), grouped[1])
            sides[b, c0] = (over, short)

        def quantise_w3(a):
            grouped = tile("w3_grouped%d" % a, [P, N * PACK], BF16)
            nc.vector.tensor_copy(
                out=grouped[:].rearrange("p (c i j) -> p c j i", i=4, j=PACK),
                in_=w3_raw[a][:].rearrange("p j (c i) -> p c j i", i=4),
            )
            return quantise("w3_%d" % a, grouped)

        groups = {}
        for h in range(2):
            for t in range(PACK):
                groups[t, h] = bank(PACK * h + t)
                supply_pass(groups[t, h], 0, t, h)
        for h in range(2):
            for t in range(PACK):
                demand_pass(groups[t, h], 0, 0, t, h)
            for t in range(PACK):
                demand_pass(groups[t, h], 1, 0, t, h)
                leave_gap(groups[t, h], 0, t, h)
        w1_q[0, 1] = quantise("w1_01", round_w1(0, 1, [nc.vector], w1_tile(0, 1)))
        w1_q[1, 1] = quantise("w1_11", round_w1(1, 1, [nc.vector], side_tile("over", PASS)), pieces=PACK)
        for h in range(2):
            for t in range(PACK):
                groups[t, h] = bank(PACK * h + t)
                supply_pass(groups[t, h], 1, t, h)
                demand_pass(groups[t, h], 0, 1, t, h)
            for t in range(PACK):
                demand_pass(groups[t, h], 1, 1, t, h)
                leave_gap(groups[t, h], 1, t, h)

        chunks = [(0, HALF), (HALF, HALF + HALF // 2), (HALF + HALF // 2, S)]
        split_gap(0, 0, HALF)
        w3_q = [quantise_w3(0)]
        split_gap(0, HALF, S)
        split_gap(1, 0, HALF)
        w3_q.append(quantise_w3(1))
        for c0, c1 in chunks[1:]:
            split_gap(1, c0, c1)

        def score_passes(group, b, i, c0, c1):
            cols = slice(i * P, (i + 1) * P)
            first = c0 if b == 1 else c0 // HALF * HALF
            (over_codes, over_plane), (short_codes, short_plane) = sides[b, first]
            w3_codes, w3_plane = w3_q[b]
            entries = slice(c0 - first, c1 - first)
            nc.tensor.matmul_mx(
                out=group[:, 0 : c1 - c0],
                lhsT=w4[:, b, cols].bitcast(FP8X4),
                lhsT_scale=w4_plane[4 * b : P, cols],
                rhs=over_codes[:, entries].bitcast(FP8X4),
                rhs_scale=over_plane[:, entries],
                start=(b == 0), stop=False,
            )
            nc.tensor.matmul_mx(
                out=group[:, 0 : c1 - c0],
                lhsT=w3_codes[:, cols].bitcast(FP8X4),
                lhsT_scale=w3_plane[:, cols],
                rhs=short_codes[:, entries].bitcast(FP8X4),
                rhs_scale=short_plane[:, entries],
                start=False, stop=(b == 1),
            )

        row_tiles = N // P
        for n, (c0, c1) in enumerate(chunks):
            scores = [bank(row_tiles * (n % 2) + i) for i in range(row_tiles)]
            for i in range(row_tiles):
                score_passes(scores[i], 0, i, c0, c1)
            for i in range(row_tiles):
                score_passes(scores[i], 1, i, c0, c1)
                result = tile("result%d_%d" % (i, c0), [P, c1 - c0], F32)
                if n == len(chunks) - 1 and i % 2 == 1:
                    nc.vector.tensor_scalar(out=result[:], in0=scores[i][:, 0 : c1 - c0], scalar1=bias[:, i : i + 1], scalar2=None, op0=ALU.add)
                else:
                    nc.scalar.activation(out=result[:], in_=scores[i][:, 0 : c1 - c0], func=ACT.Identity, bias=bias[:, i : i + 1])
                nc.sync.dma_start(out=out[i * P : (i + 1) * P, c0:c1], in_=result[:])
